import numpy as np
import ml_dtypes


def mxq(x, axis, fmt="e4m3"):
    dtype, down = {"e4m3": (ml_dtypes.float8_e4m3fn, 7), "e5m2": (ml_dtypes.float8_e5m2, 14)}[fmt]
    v = np.moveaxis(np.asarray(x, np.float32).astype(ml_dtypes.bfloat16).astype(np.float64), axis, -1)
    blocks = v.reshape(v.shape[:-1] + (-1, 32))
    amax = np.abs(blocks).max(-1, keepdims=True)
    byte = np.maximum(np.where(amax > 0, np.frexp(amax)[1] - 1 + 127, 0) - down, 1)
    scale = np.exp2(byte - 127.0)
    codes = (blocks / scale).astype(np.float32).astype(dtype).astype(np.float64)
    return np.moveaxis((codes * scale).reshape(v.shape), -1, axis)


WIDE = False


def mx_kscale(k):
    if not WIDE:
        return np.ones(k)
    levels = np.array([30, -30])
    if k % 512:
        return np.exp2(np.random.permutation(np.resize(levels, k // 32))).repeat(32)
    a = np.empty((k // 512, 16))
    for p in range(k // 512):
        a[p, :8] = np.random.permutation(np.resize(levels, 8))
        for g in range(8):
            far = levels[np.abs(levels - a[p, g]) >= 10]
            a[p, g + 8] = far[np.random.randint(len(far))]
    return np.exp2(a.ravel()).repeat(32)


def f64(x):
    return np.asarray(x).astype(np.float64)


def striped(idx):
    return np.tile(np.asarray(idx).reshape(-1, 16).T, (8, 1)).astype(np.uint16)


def unstriped(offs):
    return offs[:16].T.reshape(-1).astype(np.int64)


E2M1 = np.array([0.0, 0.5, 1.0, 1.5, 2.0, 3.0, 4.0, 6.0, -0.0, -0.5, -1.0, -1.5, -2.0, -3.0, -4.0, -6.0])


def pack_weight(w, fmt):
    k, n = w.shape
    w = f64(np.asarray(w, np.float32).astype(ml_dtypes.bfloat16)).reshape(k // 32, 32, n)
    amax = np.abs(w).max(1)
    if fmt in ("e4m3", "e5m2"):
        byte = np.frexp(amax)[1] - 1 + 127 - (7 if fmt == "e4m3" else 14)
    else:
        mant, ex = np.frexp(amax / 6.0)
        byte = np.where(mant > 0.5, ex, ex - 1) + 127
    byte = np.clip(np.where(amax > 0, byte, 1), 1, 254)
    scaled = (w * np.exp2(127.0 - byte)[:, None, :]).reshape(k, n).astype(np.float32)
    by_word = np.ascontiguousarray(scaled.reshape(k // 512, 128, 4, n).transpose(0, 1, 3, 2))
    if fmt in ("e4m3", "e5m2"):
        words = by_word.astype(ml_dtypes.float8_e4m3fn if fmt == "e4m3" else ml_dtypes.float8_e5m2).view(np.uint8)
    else:
        c = by_word.astype(ml_dtypes.float4_e2m1fn).view(np.uint8) & 0xF
        words = (c[..., 0::2] | (c[..., 1::2] << 4)).reshape(k // 512, 128, 2 * n)
    return np.ascontiguousarray(words), np.ascontiguousarray(byte.astype(np.uint8).reshape(k // 512, 16, n))


def unpack_weight(words, scales, fmt):
    g, _, n = scales.shape
    words = np.ascontiguousarray(words).reshape(g, 128, n, -1)
    if fmt in ("e4m3", "e5m2"):
        vals = words.view(ml_dtypes.float8_e4m3fn if fmt == "e4m3" else ml_dtypes.float8_e5m2).astype(np.float64)
    else:
        nib = np.empty((g, 128, n, 4), np.uint8)
        nib[..., 0::2] = words & 0xF
        nib[..., 1::2] = words >> 4
        vals = E2M1[nib]
    vals = vals * np.repeat(np.exp2(scales.astype(np.float64) - 127.0), 8, axis=1)[..., None]
    return vals.transpose(0, 1, 3, 2).reshape(g * 512, n)


K, J, N, R, T, V = 512, 512, 256, 256, 1024, 1024


def setup_inputs():
    n = np.random.standard_normal
    idx = np.random.permutation(T)[:J]
    idx2 = np.random.permutation(V)[:J]
    fj = mx_kscale(J)
    fk = mx_kscale(K)
    drp = pack_weight(n((K, R)) * 1 / np.sqrt(K) / fk[:, None], "e5m2")
    return {
        "xf": (n((K, T))).astype(np.float32),
        "ra": (np.random.uniform(0.5, 1.5, (1, J)) * fj).astype(np.float32),
        "ow": (n((K, J)) * 0.7).astype(np.float32),
        "gt": (n((N, V)) * np.exp(0.5 * n((1, V)))).astype(np.float32),
        "rb": (np.random.uniform(0.5, 1.5, (1, J)) / fj).astype(np.float32),
        "fkr": (np.random.uniform(0.5, 1.5, (1, K)) * fk).astype(np.float32),
        "dr_words": drp[0],
        "dr_scales": drp[1],
        "bn": (np.random.uniform(-12.0, 12.0, (1, N))).astype(np.float32),
        "offs": striped(idx),
        "offs2": striped(idx2),
    }


def reference(xf, ra, ow, gt, rb, fkr, dr_words, dr_scales, bn, offs, offs2):
    idx = unstriped(offs)
    idx2 = unstriped(offs2)
    dru = unpack_weight(dr_words, dr_scales, "e5m2")
    us = (f64(xf)[:, idx] - f64(ow)) * f64(ra)
    ut = us.T
    uj = ut * f64(fkr)
    gs = f64(gt)[:, idx2] * f64(rb)
    gj = gs.T
    ujq = mxq(uj, 0, "e4m3")
    gjq = mxq(gj, 0, "e5m2")
    w = ujq.T @ gjq
    wq = mxq(w, 0, "e5m2")
    v2 = dru.T @ wq
    wv = v2 + f64(bn)
    mn = np.mean(wv, axis=1, keepdims=True)
    dw = wv - mn
    y = dw / (np.mean(np.abs(dw), axis=1, keepdims=True) + 2.0)
    return y

@@ -1,0 +1,205 @@
+from contextlib import ExitStack
+
+import concourse.mybir as mybir
+from concourse.masks import make_identity
+
+K, J, N, R, T = 512, 512, 256, 256, 1024
+FLOPS = 2 * J * K * N + 2 * K * R * N
+
+F32 = mybir.dt.float32
+BF16 = mybir.dt.bfloat16
+I32 = mybir.dt.int32
+U32 = mybir.dt.uint32
+U16 = mybir.dt.uint16
+U8 = mybir.dt.uint8
+E4M3 = mybir.dt.float8_e4m3fn_x4
+E5M2 = mybir.dt.float8_e5m2_x4
+ALU = mybir.AluOpType
+ACT = mybir.ActivationFunctionType
+
+P = 128
+PACK = 4
+HALF = J // 2
+
+
+def tile_list_directions_offset_listed_spread_kernel(
+    tc, xf, ra, ow, gt, rb, fkr, dr_words, dr_scales, bn, offs, offs2, out
+):
+    nc = tc.nc
+    with ExitStack() as ctx:
+        keep = ctx.enter_context(tc.tile_pool(name="keep", bufs=1))
+        psum = ctx.enter_context(tc.psum_pool(name="psum", bufs=1))
+
+        def sb(name, shape, dtype, tag=None, bufs=1):
+            return keep.tile(shape, dtype, name=name, tag=tag or name, bufs=bufs, align_bytes=64)
+
+        x_list = sb("x_list", [P, J // 16], U16)
+        g_list = sb("g_list", [P, J // 16], U16)
+        ra4 = sb("ra4", [P, PACK], F32)
+        rb4 = sb("rb4", [P, PACK], F32)
+        fk4 = sb("fk4", [P, PACK], F32)
+        g_win = [sb("g_win%d" % h, [P, T], F32) for h in range(2)]
+        x_win = [sb("x_win%d" % t, [P, T], F32) for t in range(PACK)]
+        own = [sb("own%d" % t, [P, J], F32) for t in range(PACK)]
+        dr_c = sb("dr_c", [P, R], U32)
+        dr_s = sb("dr_s", [P, R], U8)
+        bn_bc = sb("bn_bc", [P, N], F32)
+        ident = sb("ident", [P, P], F32)
+
+        xf4 = xf.rearrange("(p t) c -> t p c", t=PACK)
+        ow4 = ow.rearrange("(p t) c -> t p c", t=PACK)
+
+        def four(row):
+            return row.rearrange("o (p t) -> (o p) t", t=PACK)
+
+        nc.sync.dma_start(g_list[:], offs2)
+        nc.sync.dma_start(g_win[0][:], gt[0:P, :])
+        nc.sync.dma_start(rb4[:], four(rb))
+        nc.sync.dma_start(g_win[1][:], gt[P : 2 * P, :])
+        nc.sync.dma_start(x_list[:], offs)
+        nc.sync.dma_start(ra4[:], four(ra))
+        nc.sync.dma_start(fk4[:], four(fkr))
+        for t in range(PACK):
+            nc.sync.dma_start(x_win[t][:], xf4[t])
+            nc.sync.dma_start(own[t][:], ow4[t])
+        nc.vector.memset(dr_s[:].bitcast(I32), 0)
+        nc.sync.dma_start(
+            dr_c[:].bitcast(I32), dr_words[0].rearrange("p c t -> p (c t)").bitcast(I32)
+        )
+        for q in range(4):
+            nc.sync.dma_start(
+                dr_s[32 * q : 32 * q + 4, :].bitcast(I32),
+                dr_scales[0, 4 * q : 4 * q + 4, :].bitcast(I32),
+            )
+        nc.sync.dma_start(bn_bc[:], bn[0].partition_broadcast(P))
+
+        make_identity(nc, ident[:])
+
+        def spread(name, v4):
+            bank = psum.tile([P, PACK, P], F32, name=name)
+            for t in range(PACK):
+                nc.tensor.transpose(bank[:, t, :], v4[:, t : t + 1].to_broadcast([P, P]), ident[:])
+            return bank[:].rearrange("p t q -> p q t")
+
+        rb_j = spread("rb_bank", rb4)
+        ra_j = spread("ra_bank", ra4)
+
+        def turn(name, rounded):
+            words = rounded[:].bitcast(F32)
+            bank = psum.tile([P, 2, P], F32, name=name + "_bank", tag="turn", bufs=2)
+            for u in range(2):
+                nc.tensor.transpose(bank[:, u, :], words[:, u : J // 2 : 2], ident[:])
+            grouped = sb(name + "_grouped", [P, P, PACK], BF16)
+            nc.scalar.copy(grouped[:].bitcast(F32), bank[:].rearrange("p u c -> p c u"))
+            return grouped
+
+        def quantise(name, grouped, fmt):
+            codes = sb(name + "_codes", [P, P], U32)
+            scales = sb(name + "_scales", [P, P], U8)
+            nc.vector.quantize_mx(
+                out=codes[:].bitcast(fmt),
+                scales=scales[:],
+                in_=grouped[:].rearrange("p c t -> p (c t)"),
+            )
+            return codes, scales
+
+        def by4(ap):
+            return ap.rearrange("p (q t) -> p q t", t=PACK)
+
+        def g_tile(h):
+            picked = sb("g_picked%d" % h, [P, J], F32)
+            nc.vector.tensor_copy(picked[:, 0:HALF], g_win[h][:].indirect(g_list[:, 0 : HALF // 16]))
+            nc.scalar.activation(
+                picked[:, HALF:J], g_win[h][:].indirect(g_list[:, HALF // 16 : J // 16]), ACT.Copy
+            )
+            rounded = sb("g_rounded%d" % h, [P, J], BF16)
+            nc.vector.tensor_tensor(by4(rounded[:]), by4(picked[:]), rb_j, ALU.mult)
+            return turn("g%d" % h, rounded)
+
+        def x_tile(t):
+            rounded = sb("x_rounded%d" % t, [P, J], BF16)
+            for a in range(2):
+                lo, hi = a * HALF, (a + 1) * HALF
+                picked = sb("x_picked%d_%d" % (t, a), [P, HALF], F32, tag="picked%d" % a)
+                nc.scalar.activation(
+                    picked[:], x_win[t][:].indirect(x_list[:, lo // 16 : hi // 16]), ACT.Copy
+                )
+                diff = sb("diff%d_%d" % (t, a), [P, HALF], F32)
+                nc.vector.tensor_tensor(diff[:], picked[:], own[t][:, lo:hi], ALU.subtract)
+                nc.vector.scalar_tensor_tensor(
+                    by4(rounded[:, lo:hi]),
+                    by4(diff[:]),
+                    fk4[:, t : t + 1],
+                    ra_j[:, lo // PACK : hi // PACK, :],
+                    ALU.mult,
+                    ALU.mult,
+                )
+            return turn("x%d" % t, rounded)
+
+        w_bank = [psum.tile([P, PACK, P], F32, name="w_bank%d" % h) for h in range(2)]
+
+        def first_product(t, uq, gq):
+            for h in range(2):
+                nc.tensor.matmul_mx(
+                    out=w_bank[h][:, t, :],
+                    lhsT=uq[0][:].bitcast(E4M3),
+                    lhsT_scale=uq[1][:],
+                    rhs=gq[h][0][:].bitcast(E5M2),
+                    rhs_scale=gq[h][1][:],
+                    start=True,
+                    stop=True,
+                )
+
+        g_grouped = [g_tile(h) for h in range(2)]
+        pending = x_tile(0)
+        gq = [quantise("g%d" % h, g_grouped[h], E5M2) for h in range(2)]
+        for t in range(PACK):
+            following = x_tile(t + 1) if t + 1 < PACK else None
+            first_product(t, quantise("u%d" % t, pending, E4M3), gq)
+            pending = following
+
+        w_grouped = [sb("w_grouped%d" % h, [P, P, PACK], BF16) for h in range(2)]
+        nc.vector.tensor_copy(w_grouped[0][:], w_bank[0][:].rearrange("p t n -> p n t"))
+        nc.scalar.copy(w_grouped[1][:], w_bank[1][:].rearrange("p t n -> p n t"))
+
+        v_bank = [psum.tile([P, N], F32, name="v_bank%d" % b) for b in range(2)]
+        for h in (1, 0):
+            codes, scales = quantise("w%d" % h, w_grouped[h], E5M2)
+            for b in range(2):
+                nc.tensor.matmul_mx(
+                    out=v_bank[b][:, h * P : (h + 1) * P],
+                    lhsT=dr_c[:, b * P : (b + 1) * P].bitcast(E5M2),
+                    lhsT_scale=dr_s[:, b * P : (b + 1) * P],
+                    rhs=codes[:].bitcast(E5M2),
+                    rhs_scale=scales[:],
+                    start=True,
+                    stop=True,
+                )
+
+        wv = [sb("wv%d" % b, [P, N], F32) for b in range(2)]
+        total = [sb("total%d" % b, [P, 1], F32) for b in range(2)]
+        mag = [sb("mag%d" % b, [P, N], F32) for b in range(2)]
+        mag_sum = [sb("mag_sum%d" % b, [P, 1], F32) for b in range(2)]
+        mean = [sb("mean%d" % b, [P, 1], F32) for b in range(2)]
+        den = [sb("den%d" % b, [P, 1], F32) for b in range(2)]
+        inv = [sb("inv%d" % b, [P, 1], F32) for b in range(2)]
+        res = [sb("res%d" % b, [P, N], F32) for b in range(2)]
+        for b in range(2):
+            nc.vector.scalar_tensor_tensor(
+                wv[b][:], v_bank[b][:], 1.0, bn_bc[:], ALU.mult, ALU.add, accum_out=total[b][:]
+            )
+            nc.scalar.activation(
+                mag[b][:], wv[b][:], ACT.Abs, bias=total[b][:], scale=-float(N),
+                accum_out=mag_sum[b][:],
+            )
+        for b in range(2):
+            nc.vector.tensor_scalar(
+                den[b][:], mag_sum[b][:], 1.0 / (N * N), 2.0, ALU.mult, ALU.add
+            )
+            nc.vector.tensor_scalar(mean[b][:], total[b][:], 1.0 / N, None, ALU.mult)
+            nc.vector.reciprocal(inv[b][:], den[b][:])
+        for b in range(2):
+            nc.vector.tensor_scalar(
+                res[b][:], wv[b][:], mean[b][:], inv[b][:], ALU.subtract, ALU.mult
+            )
+            nc.sync.dma_start(out[b * P : (b + 1) * P, :], res[b][:])

@@ -20,6 +20,8 @@ ACT = mybir.ActivationFunctionType
 P = 128
 PACK = 4
 HALF = J // 2
+CUTS = ((0, HALF, J),) * 4
+FUSED = (True,) * 4
 
 
 def tile_list_directions_offset_listed_spread_kernel(
@@ -52,16 +54,21 @@ def tile_list_directions_offset_listed_spread_kernel(
         def four(row):
             return row.rearrange("o (p t) -> (o p) t", t=PACK)
 
+        def load_x(t):
+            nc.sync.dma_start(own[t][:], ow4[t])
+            nc.sync.dma_start(x_win[t][:], xf4[t])
+
+        nc.sync.dma_start(x_list[:], offs)
+        load_x(0)
+        nc.sync.dma_start(ra4[:], four(ra))
+        nc.sync.dma_start(fk4[:], four(fkr))
         nc.sync.dma_start(g_list[:], offs2)
         nc.sync.dma_start(g_win[0][:], gt[0:P, :])
         nc.sync.dma_start(rb4[:], four(rb))
+        load_x(1)
         nc.sync.dma_start(g_win[1][:], gt[P : 2 * P, :])
-        nc.sync.dma_start(x_list[:], offs)
-        nc.sync.dma_start(ra4[:], four(ra))
-        nc.sync.dma_start(fk4[:], four(fkr))
-        for t in range(PACK):
-            nc.sync.dma_start(x_win[t][:], xf4[t])
-            nc.sync.dma_start(own[t][:], ow4[t])
+        load_x(2)
+        load_x(3)
         nc.vector.memset(dr_s[:].bitcast(I32), 0)
         nc.sync.dma_start(
             dr_c[:].bitcast(I32), dr_words[0].rearrange("p c t -> p (c t)").bitcast(I32)
@@ -73,6 +80,9 @@ def tile_list_directions_offset_listed_spread_kernel(
             )
         nc.sync.dma_start(bn_bc[:], bn[0].partition_broadcast(P))
 
+        warm = sb("warm", [P, 2], F32)
+        nc.vector.memset(warm[:, 0:1], 0.0)
+        nc.scalar.activation(warm[:, 1:2], warm[:, 0:1], ACT.Abs)
         make_identity(nc, ident[:])
 
         def spread(name, v4):
@@ -81,97 +91,112 @@ def tile_list_directions_offset_listed_spread_kernel(
                 nc.tensor.transpose(bank[:, t, :], v4[:, t : t + 1].to_broadcast([P, P]), ident[:])
             return bank[:].rearrange("p t q -> p q t")
 
-        rb_j = spread("rb_bank", rb4)
         ra_j = spread("ra_bank", ra4)
+        rb_j = spread("rb_bank", rb4)
 
-        def turn(name, rounded):
-            words = rounded[:].bitcast(F32)
-            bank = psum.tile([P, 2, P], F32, name=name + "_bank", tag="turn", bufs=2)
-            for u in range(2):
-                nc.tensor.transpose(bank[:, u, :], words[:, u : J // 2 : 2], ident[:])
-            grouped = sb(name + "_grouped", [P, P, PACK], BF16)
-            nc.scalar.copy(grouped[:].bitcast(F32), bank[:].rearrange("p u c -> p c u"))
+        def turn(name, tiles, tag):
+            n = len(tiles)
+            bank = psum.tile([P, n, 2, P], F32, name=name + "_bank", tag="turn", bufs=2)
+            for i, rounded in enumerate(tiles):
+                words = rounded[:].bitcast(F32)
+                for u in range(2):
+                    nc.tensor.transpose(bank[:, i, u, :], words[:, u : J // 2 : 2], ident[:])
+            grouped = sb(name + "_grouped", [P, n, P, PACK], BF16, tag=tag)
+            nc.scalar.copy(grouped[:].bitcast(F32), bank[:].rearrange("p i u c -> p i c u"))
             return grouped
 
-        def quantise(name, grouped, fmt):
-            codes = sb(name + "_codes", [P, P], U32)
-            scales = sb(name + "_scales", [P, P], U8)
+        def quantise(name, grouped, fmt, scales):
+            n = grouped.shape[1]
+            codes = sb(name + "_codes", [P, n, P], U32)
             nc.vector.quantize_mx(
-                out=codes[:].bitcast(fmt),
-                scales=scales[:],
-                in_=grouped[:].rearrange("p c t -> p (c t)"),
+                out=codes[:].rearrange("p i c -> p (i c)").bitcast(fmt),
+                scales=scales.rearrange("p i c -> p (i c)"),
+                in_=grouped[:].rearrange("p i c t -> p (i c t)"),
             )
-            return codes, scales
+            return [(codes[:, i, :], scales[:, i, :]) for i in range(n)]
 
         def by4(ap):
             return ap.rearrange("p (q t) -> p q t", t=PACK)
 
         def g_tile(h):
             picked = sb("g_picked%d" % h, [P, J], F32)
-            nc.vector.tensor_copy(picked[:, 0:HALF], g_win[h][:].indirect(g_list[:, 0 : HALF // 16]))
-            nc.scalar.activation(
-                picked[:, HALF:J], g_win[h][:].indirect(g_list[:, HALF // 16 : J // 16]), ACT.Copy
-            )
+            nc.scalar.activation(picked[:], g_win[h][:].indirect(g_list[:]), ACT.Copy)
             rounded = sb("g_rounded%d" % h, [P, J], BF16)
             nc.vector.tensor_tensor(by4(rounded[:]), by4(picked[:]), rb_j, ALU.mult)
-            return turn("g%d" % h, rounded)
+            return rounded
 
         def x_tile(t):
             rounded = sb("x_rounded%d" % t, [P, J], BF16)
-            for a in range(2):
-                lo, hi = a * HALF, (a + 1) * HALF
-                picked = sb("x_picked%d_%d" % (t, a), [P, HALF], F32, tag="picked%d" % a)
-                nc.scalar.activation(
-                    picked[:], x_win[t][:].indirect(x_list[:, lo // 16 : hi // 16]), ACT.Copy
-                )
-                diff = sb("diff%d_%d" % (t, a), [P, HALF], F32)
-                nc.vector.tensor_tensor(diff[:], picked[:], own[t][:, lo:hi], ALU.subtract)
+            cuts = CUTS[t]
+            diffs = []
+            for a, (lo, hi) in enumerate(zip(cuts, cuts[1:])):
+                diff = sb("diff%d_%d" % (t, a), [P, hi - lo], F32, tag="diff%d" % a)
+                listed = x_win[t][:].indirect(x_list[:, lo // 16 : hi // 16])
+                if a == 0 and FUSED[t]:
+                    nc.vector.tensor_tensor(diff[:], listed, own[t][:, lo:hi], ALU.subtract)
+                else:
+                    picked = sb("x_picked%d_%d" % (t, a), [P, hi - lo], F32)
+                    nc.scalar.activation(picked[:], listed, ACT.Copy)
+                    nc.vector.tensor_tensor(diff[:], picked[:], own[t][:, lo:hi], ALU.subtract)
+                diffs.append(diff)
+            for a, (lo, hi) in enumerate(zip(cuts, cuts[1:])):
                 nc.vector.scalar_tensor_tensor(
                     by4(rounded[:, lo:hi]),
-                    by4(diff[:]),
+                    by4(diffs[a][:]),
                     fk4[:, t : t + 1],
                     ra_j[:, lo // PACK : hi // PACK, :],
                     ALU.mult,
                     ALU.mult,
                 )
-            return turn("x%d" % t, rounded)
+            return rounded
 
         w_bank = [psum.tile([P, PACK, P], F32, name="w_bank%d" % h) for h in range(2)]
 
-        def first_product(t, uq, gq):
-            for h in range(2):
-                nc.tensor.matmul_mx(
-                    out=w_bank[h][:, t, :],
-                    lhsT=uq[0][:].bitcast(E4M3),
-                    lhsT_scale=uq[1][:],
-                    rhs=gq[h][0][:].bitcast(E5M2),
-                    rhs_scale=gq[h][1][:],
-                    start=True,
-                    stop=True,
-                )
+        def first_product(t, h, uq, gq):
+            nc.tensor.matmul_mx(
+                out=w_bank[h][:, t, :],
+                lhsT=uq[0].bitcast(E4M3),
+                lhsT_scale=uq[1],
+                rhs=gq[0].bitcast(E5M2),
+                rhs_scale=gq[1],
+                start=True,
+                stop=True,
+            )
 
-        g_grouped = [g_tile(h) for h in range(2)]
-        pending = x_tile(0)
-        gq = [quantise("g%d" % h, g_grouped[h], E5M2) for h in range(2)]
+        x0 = x_tile(0)
+        g0 = g_tile(0)
+        x1 = x_tile(1)
+        g1 = g_tile(1)
+        x2 = x_tile(2)
+        x01 = turn("x01", [x0, x1], "x_win2")
+        x3 = x_tile(3)
+        g01 = turn("g01", [g0, g1], "x_win3")
+        x2 = turn("x2", [x2], "x_picked3_1")
+        x3 = turn("x3", [x3], None)
+        scales = sb("first_scales", [P, 6, P], U8, tag="diff1")
+        uq = quantise("u01", x01, E4M3, scales[:, 0:2, :])
+        gq = quantise("g01", g01, E5M2, scales[:, 2:4, :])
+        uq = uq + quantise("u2", x2, E4M3, scales[:, 4:5, :])
+        uq = uq + quantise("u3", x3, E4M3, scales[:, 5:6, :])
         for t in range(PACK):
-            following = x_tile(t + 1) if t + 1 < PACK else None
-            first_product(t, quantise("u%d" % t, pending, E4M3), gq)
-            pending = following
+            for h in range(2):
+                first_product(t, h, uq[t], gq[h])
 
-        w_grouped = [sb("w_grouped%d" % h, [P, P, PACK], BF16) for h in range(2)]
-        nc.vector.tensor_copy(w_grouped[0][:], w_bank[0][:].rearrange("p t n -> p n t"))
-        nc.scalar.copy(w_grouped[1][:], w_bank[1][:].rearrange("p t n -> p n t"))
+        w_grouped = [sb("w_grouped%d" % h, [P, 1, P, PACK], BF16) for h in range(2)]
+        nc.vector.tensor_copy(w_grouped[0][:, 0], w_bank[0][:].rearrange("p t n -> p n t"))
+        nc.scalar.copy(w_grouped[1][:, 0], w_bank[1][:].rearrange("p t n -> p n t"))
 
         v_bank = [psum.tile([P, N], F32, name="v_bank%d" % b) for b in range(2)]
         for h in (1, 0):
-            codes, scales = quantise("w%d" % h, w_grouped[h], E5M2)
+            w_scales = sb("w_scales%d" % h, [P, 1, P], U8)
+            codes, scales = quantise("w%d" % h, w_grouped[h], E5M2, w_scales[:])[0]
             for b in range(2):
                 nc.tensor.matmul_mx(
                     out=v_bank[b][:, h * P : (h + 1) * P],
                     lhsT=dr_c[:, b * P : (b + 1) * P].bitcast(E5M2),
                     lhsT_scale=dr_s[:, b * P : (b + 1) * P],
-                    rhs=codes[:].bitcast(E5M2),
-                    rhs_scale=scales[:],
+                    rhs=codes.bitcast(E5M2),
+                    rhs_scale=scales,
                     start=True,
                     stop=True,
                 )

@@ -20,8 +20,8 @@ ACT = mybir.ActivationFunctionType
 P = 128
 PACK = 4
 HALF = J // 2
-CUTS = ((0, HALF, J),) * 4
-FUSED = (True,) * 4
+CUTS = ((0, J),) + ((0, HALF, J),) * 3
+FUSED = (True, True, True, False)
 
 
 def tile_list_directions_offset_listed_spread_kernel(
@@ -45,6 +45,7 @@ def tile_list_directions_offset_listed_spread_kernel(
         own = [sb("own%d" % t, [P, J], F32) for t in range(PACK)]
         dr_c = sb("dr_c", [P, R], U32)
         dr_s = sb("dr_s", [P, R], U8)
+        bn2 = sb("bn2", [P, 2], F32)
         bn_bc = sb("bn_bc", [P, N], F32)
         ident = sb("ident", [P, P], F32)
 
@@ -54,21 +55,22 @@ def tile_list_directions_offset_listed_spread_kernel(
         def four(row):
             return row.rearrange("o (p t) -> (o p) t", t=PACK)
 
-        def load_x(t):
-            nc.sync.dma_start(own[t][:], ow4[t])
-            nc.sync.dma_start(x_win[t][:], xf4[t])
-
+        nc.sync.dma_start(bn2[:], bn.rearrange("o (p t) -> (o p) t", t=2))
         nc.sync.dma_start(x_list[:], offs)
-        load_x(0)
+        nc.sync.dma_start(own[0][:], ow4[0])
+        nc.sync.dma_start(x_win[0][:], xf4[0])
         nc.sync.dma_start(ra4[:], four(ra))
         nc.sync.dma_start(fk4[:], four(fkr))
         nc.sync.dma_start(g_list[:], offs2)
         nc.sync.dma_start(g_win[0][:], gt[0:P, :])
         nc.sync.dma_start(rb4[:], four(rb))
-        load_x(1)
+        nc.sync.dma_start(own[1][:], ow4[1])
+        nc.sync.dma_start(x_win[1][:], xf4[1])
         nc.sync.dma_start(g_win[1][:], gt[P : 2 * P, :])
-        load_x(2)
-        load_x(3)
+        nc.sync.dma_start(own[2][:], ow4[2])
+        nc.sync.dma_start(x_win[2][:], xf4[2])
+        nc.sync.dma_start(x_win[3][:], xf4[3])
+        nc.sync.dma_start(own[3][:], ow4[3])
         nc.vector.memset(dr_s[:].bitcast(I32), 0)
         nc.sync.dma_start(
             dr_c[:].bitcast(I32), dr_words[0].rearrange("p c t -> p (c t)").bitcast(I32)
@@ -78,19 +80,18 @@ def tile_list_directions_offset_listed_spread_kernel(
                 dr_s[32 * q : 32 * q + 4, :].bitcast(I32),
                 dr_scales[0, 4 * q : 4 * q + 4, :].bitcast(I32),
             )
-        nc.sync.dma_start(bn_bc[:], bn[0].partition_broadcast(P))
 
-        warm = sb("warm", [P, 2], F32)
-        nc.vector.memset(warm[:, 0:1], 0.0)
-        nc.scalar.activation(warm[:, 1:2], warm[:, 0:1], ACT.Abs)
         make_identity(nc, ident[:])
 
-        def spread(name, v4):
-            bank = psum.tile([P, PACK, P], F32, name=name)
-            for t in range(PACK):
+        def spread(name, v4, tag=None):
+            bank = psum.tile([P, v4.shape[1], P], F32, name=name, tag=tag or name)
+            for t in range(v4.shape[1]):
                 nc.tensor.transpose(bank[:, t, :], v4[:, t : t + 1].to_broadcast([P, P]), ident[:])
             return bank[:].rearrange("p t q -> p q t")
 
+        nc.scalar.activation(
+            bn_bc[:].rearrange("p (q t) -> p q t", t=2), spread("bn_bank", bn2, "v_bank1"), ACT.Copy
+        )
         ra_j = spread("ra_bank", ra4)
         rb_j = spread("rb_bank", rb4)
 
@@ -130,7 +131,7 @@ def tile_list_directions_offset_listed_spread_kernel(
             cuts = CUTS[t]
             diffs = []
             for a, (lo, hi) in enumerate(zip(cuts, cuts[1:])):
-                diff = sb("diff%d_%d" % (t, a), [P, hi - lo], F32, tag="diff%d" % a)
+                diff = sb("diff%d_%d" % (t, a), [P, hi - lo], F32)
                 listed = x_win[t][:].indirect(x_list[:, lo // 16 : hi // 16])
                 if a == 0 and FUSED[t]:
                     nc.vector.tensor_tensor(diff[:], listed, own[t][:, lo:hi], ALU.subtract)
@@ -168,12 +169,12 @@ def tile_list_directions_offset_listed_spread_kernel(
         x1 = x_tile(1)
         g1 = g_tile(1)
         x2 = x_tile(2)
-        x01 = turn("x01", [x0, x1], "x_win2")
         x3 = x_tile(3)
-        g01 = turn("g01", [g0, g1], "x_win3")
+        x01 = turn("x01", [x0, x1], "x_win3")
+        g01 = turn("g01", [g0, g1], "x_picked3_0")
         x2 = turn("x2", [x2], "x_picked3_1")
         x3 = turn("x3", [x3], None)
-        scales = sb("first_scales", [P, 6, P], U8, tag="diff1")
+        scales = sb("first_scales", [P, 6, P], U8, tag="diff3_1")
         uq = quantise("u01", x01, E4M3, scales[:, 0:2, :])
         gq = quantise("g01", g01, E5M2, scales[:, 2:4, :])
         uq = uq + quantise("u2", x2, E4M3, scales[:, 4:5, :])

@@ -19,9 +19,11 @@ ACT = mybir.ActivationFunctionType
 
 P = 128
 PACK = 4
+LIST_ROWS = 16
 HALF = J // 2
+
 CUTS = ((0, J),) + ((0, HALF, J),) * 3
-FUSED = (True, True, True, False)
+VECTOR_GATHERS_FIRST_PART = (True, True, True, False)
 
 
 def tile_list_directions_offset_listed_spread_kernel(
@@ -32,11 +34,11 @@ def tile_list_directions_offset_listed_spread_kernel(
         keep = ctx.enter_context(tc.tile_pool(name="keep", bufs=1))
         psum = ctx.enter_context(tc.psum_pool(name="psum", bufs=1))
 
-        def sb(name, shape, dtype, tag=None, bufs=1):
-            return keep.tile(shape, dtype, name=name, tag=tag or name, bufs=bufs, align_bytes=64)
+        def sb(name, shape, dtype, tag=None):
+            return keep.tile(shape, dtype, name=name, tag=tag or name, bufs=1, align_bytes=64)
 
-        x_list = sb("x_list", [P, J // 16], U16)
-        g_list = sb("g_list", [P, J // 16], U16)
+        x_list = sb("x_list", [P, J // LIST_ROWS], U16)
+        g_list = sb("g_list", [P, J // LIST_ROWS], U16)
         ra4 = sb("ra4", [P, PACK], F32)
         rb4 = sb("rb4", [P, PACK], F32)
         fk4 = sb("fk4", [P, PACK], F32)
@@ -45,25 +47,26 @@ def tile_list_directions_offset_listed_spread_kernel(
         own = [sb("own%d" % t, [P, J], F32) for t in range(PACK)]
         dr_c = sb("dr_c", [P, R], U32)
         dr_s = sb("dr_s", [P, R], U8)
-        bn2 = sb("bn2", [P, 2], F32)
+        bn2 = sb("bn2", [P, N // P], F32)
         bn_bc = sb("bn_bc", [P, N], F32)
         ident = sb("ident", [P, P], F32)
 
         xf4 = xf.rearrange("(p t) c -> t p c", t=PACK)
         ow4 = ow.rearrange("(p t) c -> t p c", t=PACK)
 
-        def four(row):
-            return row.rearrange("o (p t) -> (o p) t", t=PACK)
+        def dealt(row, each):
+            return row.rearrange("o (p t) -> (o p) t", t=each)
 
-        nc.sync.dma_start(bn2[:], bn.rearrange("o (p t) -> (o p) t", t=2))
+        nc.scalar.dma_start(bn2[:], dealt(bn, N // P))
+        nc.scalar.dma_start(ra4[:], dealt(ra, PACK))
+        nc.scalar.dma_start(fk4[:], dealt(fkr, PACK))
+        nc.scalar.dma_start(rb4[:], dealt(rb, PACK))
+
         nc.sync.dma_start(x_list[:], offs)
         nc.sync.dma_start(own[0][:], ow4[0])
         nc.sync.dma_start(x_win[0][:], xf4[0])
-        nc.sync.dma_start(ra4[:], four(ra))
-        nc.sync.dma_start(fk4[:], four(fkr))
         nc.sync.dma_start(g_list[:], offs2)
         nc.sync.dma_start(g_win[0][:], gt[0:P, :])
-        nc.sync.dma_start(rb4[:], four(rb))
         nc.sync.dma_start(own[1][:], ow4[1])
         nc.sync.dma_start(x_win[1][:], xf4[1])
         nc.sync.dma_start(g_win[1][:], gt[P : 2 * P, :])
@@ -71,6 +74,7 @@ def tile_list_directions_offset_listed_spread_kernel(
         nc.sync.dma_start(x_win[2][:], xf4[2])
         nc.sync.dma_start(x_win[3][:], xf4[3])
         nc.sync.dma_start(own[3][:], ow4[3])
+
         nc.vector.memset(dr_s[:].bitcast(I32), 0)
         nc.sync.dma_start(
             dr_c[:].bitcast(I32), dr_words[0].rearrange("p c t -> p (c t)").bitcast(I32)
@@ -83,38 +87,43 @@ def tile_list_directions_offset_listed_spread_kernel(
 
         make_identity(nc, ident[:])
 
-        def spread(name, v4, tag=None):
-            bank = psum.tile([P, v4.shape[1], P], F32, name=name, tag=tag or name)
-            for t in range(v4.shape[1]):
-                nc.tensor.transpose(bank[:, t, :], v4[:, t : t + 1].to_broadcast([P, P]), ident[:])
+        def spread(name, columns, tag=None):
+            each = columns.shape[1]
+            bank = psum.tile([P, each, P], F32, name=name, tag=tag or name)
+            for t in range(each):
+                nc.tensor.transpose(
+                    bank[:, t, :], columns[:, t : t + 1].to_broadcast([P, P]), ident[:]
+                )
             return bank[:].rearrange("p t q -> p q t")
 
         nc.scalar.activation(
-            bn_bc[:].rearrange("p (q t) -> p q t", t=2), spread("bn_bank", bn2, "v_bank1"), ACT.Copy
+            bn_bc[:].rearrange("p (q t) -> p q t", t=N // P),
+            spread("bn_bank", bn2, "v_bank1"),
+            ACT.Copy,
         )
         ra_j = spread("ra_bank", ra4)
         rb_j = spread("rb_bank", rb4)
 
         def turn(name, tiles, tag):
-            n = len(tiles)
-            bank = psum.tile([P, n, 2, P], F32, name=name + "_bank", tag="turn", bufs=2)
+            count = len(tiles)
+            bank = psum.tile([P, count, 2, P], F32, name=name + "_bank", tag="turn", bufs=2)
             for i, rounded in enumerate(tiles):
                 words = rounded[:].bitcast(F32)
                 for u in range(2):
                     nc.tensor.transpose(bank[:, i, u, :], words[:, u : J // 2 : 2], ident[:])
-            grouped = sb(name + "_grouped", [P, n, P, PACK], BF16, tag=tag)
+            grouped = sb(name + "_grouped", [P, count, P, PACK], BF16, tag=tag)
             nc.scalar.copy(grouped[:].bitcast(F32), bank[:].rearrange("p i u c -> p i c u"))
             return grouped
 
         def quantise(name, grouped, fmt, scales):
-            n = grouped.shape[1]
-            codes = sb(name + "_codes", [P, n, P], U32)
+            count = grouped.shape[1]
+            codes = sb(name + "_codes", [P, count, P], U32)
             nc.vector.quantize_mx(
                 out=codes[:].rearrange("p i c -> p (i c)").bitcast(fmt),
                 scales=scales.rearrange("p i c -> p (i c)"),
                 in_=grouped[:].rearrange("p i c t -> p (i c t)"),
             )
-            return [(codes[:, i, :], scales[:, i, :]) for i in range(n)]
+            return [(codes[:, i, :], scales[:, i, :]) for i in range(count)]
 
         def by4(ap):
             return ap.rearrange("p (q t) -> p q t", t=PACK)
@@ -128,19 +137,19 @@ def tile_list_directions_offset_listed_spread_kernel(
 
         def x_tile(t):
             rounded = sb("x_rounded%d" % t, [P, J], BF16)
-            cuts = CUTS[t]
+            parts = list(zip(CUTS[t], CUTS[t][1:]))
             diffs = []
-            for a, (lo, hi) in enumerate(zip(cuts, cuts[1:])):
+            for a, (lo, hi) in enumerate(parts):
                 diff = sb("diff%d_%d" % (t, a), [P, hi - lo], F32)
-                listed = x_win[t][:].indirect(x_list[:, lo // 16 : hi // 16])
-                if a == 0 and FUSED[t]:
+                listed = x_win[t][:].indirect(x_list[:, lo // LIST_ROWS : hi // LIST_ROWS])
+                if a == 0 and VECTOR_GATHERS_FIRST_PART[t]:
                     nc.vector.tensor_tensor(diff[:], listed, own[t][:, lo:hi], ALU.subtract)
                 else:
                     picked = sb("x_picked%d_%d" % (t, a), [P, hi - lo], F32)
                     nc.scalar.activation(picked[:], listed, ACT.Copy)
                     nc.vector.tensor_tensor(diff[:], picked[:], own[t][:, lo:hi], ALU.subtract)
                 diffs.append(diff)
-            for a, (lo, hi) in enumerate(zip(cuts, cuts[1:])):
+            for a, (lo, hi) in enumerate(parts):
                 nc.vector.scalar_tensor_tensor(
                     by4(rounded[:, lo:hi]),
                     by4(diffs[a][:]),
@@ -153,35 +162,33 @@ def tile_list_directions_offset_listed_spread_kernel(
 
         w_bank = [psum.tile([P, PACK, P], F32, name="w_bank%d" % h) for h in range(2)]
 
-        def first_product(t, h, uq, gq):
-            nc.tensor.matmul_mx(
-                out=w_bank[h][:, t, :],
-                lhsT=uq[0].bitcast(E4M3),
-                lhsT_scale=uq[1],
-                rhs=gq[0].bitcast(E5M2),
-                rhs_scale=gq[1],
-                start=True,
-                stop=True,
-            )
-
         x0 = x_tile(0)
         g0 = g_tile(0)
         x1 = x_tile(1)
         g1 = g_tile(1)
         x2 = x_tile(2)
         x3 = x_tile(3)
-        x01 = turn("x01", [x0, x1], "x_win3")
-        g01 = turn("g01", [g0, g1], "x_picked3_0")
-        x2 = turn("x2", [x2], "x_picked3_1")
-        x3 = turn("x3", [x3], None)
-        scales = sb("first_scales", [P, 6, P], U8, tag="diff3_1")
-        uq = quantise("u01", x01, E4M3, scales[:, 0:2, :])
-        gq = quantise("g01", g01, E5M2, scales[:, 2:4, :])
-        uq = uq + quantise("u2", x2, E4M3, scales[:, 4:5, :])
-        uq = uq + quantise("u3", x3, E4M3, scales[:, 5:6, :])
+
+        x01_grouped = turn("x01", [x0, x1], "x_win3")
+        g01_grouped = turn("g01", [g0, g1], "x_picked3_0")
+        x2_grouped = turn("x2", [x2], "x_picked3_1")
+        x3_grouped = turn("x3", [x3], None)
+        first_scales = sb("first_scales", [P, PACK + 2, P], U8, tag="diff3_1")
+        uq = quantise("u01", x01_grouped, E4M3, first_scales[:, 0:2, :])
+        gq = quantise("g01", g01_grouped, E5M2, first_scales[:, 2:4, :])
+        uq = uq + quantise("u2", x2_grouped, E4M3, first_scales[:, 4:5, :])
+        uq = uq + quantise("u3", x3_grouped, E4M3, first_scales[:, 5:6, :])
         for t in range(PACK):
             for h in range(2):
-                first_product(t, h, uq[t], gq[h])
+                nc.tensor.matmul_mx(
+                    out=w_bank[h][:, t, :],
+                    lhsT=uq[t][0].bitcast(E4M3),
+                    lhsT_scale=uq[t][1],
+                    rhs=gq[h][0].bitcast(E5M2),
+                    rhs_scale=gq[h][1],
+                    start=True,
+                    stop=True,
+                )
 
         w_grouped = [sb("w_grouped%d" % h, [P, 1, P, PACK], BF16) for h in range(2)]
         nc.vector.tensor_copy(w_grouped[0][:, 0], w_bank[0][:].rearrange("p t n -> p n t"))
@@ -190,14 +197,14 @@ def tile_list_directions_offset_listed_spread_kernel(
         v_bank = [psum.tile([P, N], F32, name="v_bank%d" % b) for b in range(2)]
         for h in (1, 0):
             w_scales = sb("w_scales%d" % h, [P, 1, P], U8)
-            codes, scales = quantise("w%d" % h, w_grouped[h], E5M2, w_scales[:])[0]
+            w_codes, w_bytes = quantise("w%d" % h, w_grouped[h], E5M2, w_scales[:])[0]
             for b in range(2):
                 nc.tensor.matmul_mx(
                     out=v_bank[b][:, h * P : (h + 1) * P],
                     lhsT=dr_c[:, b * P : (b + 1) * P].bitcast(E5M2),
                     lhsT_scale=dr_s[:, b * P : (b + 1) * P],
-                    rhs=codes.bitcast(E5M2),
-                    rhs_scale=scales,
+                    rhs=w_codes.bitcast(E5M2),
+                    rhs_scale=w_bytes,
                     start=True,
                     stop=True,
                 )
@@ -215,7 +222,11 @@ def tile_list_directions_offset_listed_spread_kernel(
                 wv[b][:], v_bank[b][:], 1.0, bn_bc[:], ALU.mult, ALU.add, accum_out=total[b][:]
             )
             nc.scalar.activation(
-                mag[b][:], wv[b][:], ACT.Abs, bias=total[b][:], scale=-float(N),
+                mag[b][:],
+                wv[b][:],
+                ACT.Abs,
+                bias=total[b][:],
+                scale=-float(N),
                 accum_out=mag_sum[b][:],
             )
         for b in range(2):

from contextlib import ExitStack

import concourse.mybir as mybir
from concourse.masks import make_identity

K, J, N, R, T = 512, 512, 256, 256, 1024
FLOPS = 2 * J * K * N + 2 * K * R * N

F32 = mybir.dt.float32
BF16 = mybir.dt.bfloat16
I32 = mybir.dt.int32
U32 = mybir.dt.uint32
U16 = mybir.dt.uint16
U8 = mybir.dt.uint8
E4M3 = mybir.dt.float8_e4m3fn_x4
E5M2 = mybir.dt.float8_e5m2_x4
ALU = mybir.AluOpType
ACT = mybir.ActivationFunctionType

P = 128
PACK = 4
LIST_ROWS = 16
HALF = J // 2

CUTS = ((0, J),) + ((0, HALF, J),) * 3
VECTOR_GATHERS_FIRST_PART = (True, True, True, False)


def tile_list_directions_offset_listed_spread_kernel(
    tc, xf, ra, ow, gt, rb, fkr, dr_words, dr_scales, bn, offs, offs2, out
):
    nc = tc.nc
    with ExitStack() as ctx:
        keep = ctx.enter_context(tc.tile_pool(name="keep", bufs=1))
        psum = ctx.enter_context(tc.psum_pool(name="psum", bufs=1))

        def sb(name, shape, dtype, tag=None):
            return keep.tile(shape, dtype, name=name, tag=tag or name, bufs=1, align_bytes=64)

        x_list = sb("x_list", [P, J // LIST_ROWS], U16)
        g_list = sb("g_list", [P, J // LIST_ROWS], U16)
        ra4 = sb("ra4", [P, PACK], F32)
        rb4 = sb("rb4", [P, PACK], F32)
        fk4 = sb("fk4", [P, PACK], F32)
        g_win = [sb("g_win%d" % h, [P, T], F32) for h in range(2)]
        x_win = [sb("x_win%d" % t, [P, T], F32) for t in range(PACK)]
        own = [sb("own%d" % t, [P, J], F32) for t in range(PACK)]
        dr_c = sb("dr_c", [P, R], U32)
        dr_s = sb("dr_s", [P, R], U8)
        bn2 = sb("bn2", [P, N // P], F32)
        bn_bc = sb("bn_bc", [P, N], F32)
        ident = sb("ident", [P, P], F32)

        xf4 = xf.rearrange("(p t) c -> t p c", t=PACK)
        ow4 = ow.rearrange("(p t) c -> t p c", t=PACK)

        def dealt(row, each):
            return row.rearrange("o (p t) -> (o p) t", t=each)

        nc.scalar.dma_start(bn2[:], dealt(bn, N // P))
        nc.scalar.dma_start(ra4[:], dealt(ra, PACK))
        nc.scalar.dma_start(fk4[:], dealt(fkr, PACK))
        nc.scalar.dma_start(rb4[:], dealt(rb, PACK))

        nc.sync.dma_start(x_list[:], offs)
        nc.sync.dma_start(own[0][:], ow4[0])
        nc.sync.dma_start(x_win[0][:], xf4[0])
        nc.sync.dma_start(g_list[:], offs2)
        nc.sync.dma_start(g_win[0][:], gt[0:P, :])
        nc.sync.dma_start(own[1][:], ow4[1])
        nc.sync.dma_start(x_win[1][:], xf4[1])
        nc.sync.dma_start(g_win[1][:], gt[P : 2 * P, :])
        nc.sync.dma_start(own[2][:], ow4[2])
        nc.sync.dma_start(x_win[2][:], xf4[2])
        nc.sync.dma_start(x_win[3][:], xf4[3])
        nc.sync.dma_start(own[3][:], ow4[3])

        nc.vector.memset(dr_s[:].bitcast(I32), 0)
        nc.sync.dma_start(
            dr_c[:].bitcast(I32), dr_words[0].rearrange("p c t -> p (c t)").bitcast(I32)
        )
        for q in range(4):
            nc.sync.dma_start(
                dr_s[32 * q : 32 * q + 4, :].bitcast(I32),
                dr_scales[0, 4 * q : 4 * q + 4, :].bitcast(I32),
            )

        make_identity(nc, ident[:])

        def spread(name, columns, tag=None):
            each = columns.shape[1]
            bank = psum.tile([P, each, P], F32, name=name, tag=tag or name)
            for t in range(each):
                nc.tensor.transpose(
                    bank[:, t, :], columns[:, t : t + 1].to_broadcast([P, P]), ident[:]
                )
            return bank[:].rearrange("p t q -> p q t")

        nc.scalar.activation(
            bn_bc[:].rearrange("p (q t) -> p q t", t=N // P),
            spread("bn_bank", bn2, "v_bank1"),
            ACT.Copy,
        )
        ra_j = spread("ra_bank", ra4)
        rb_j = spread("rb_bank", rb4)

        def turn(name, tiles, tag):
            count = len(tiles)
            bank = psum.tile([P, count, 2, P], F32, name=name + "_bank", tag="turn", bufs=2)
            for i, rounded in enumerate(tiles):
                words = rounded[:].bitcast(F32)
                for u in range(2):
                    nc.tensor.transpose(bank[:, i, u, :], words[:, u : J // 2 : 2], ident[:])
            grouped = sb(name + "_grouped", [P, count, P, PACK], BF16, tag=tag)
            nc.scalar.copy(grouped[:].bitcast(F32), bank[:].rearrange("p i u c -> p i c u"))
            return grouped

        def quantise(name, grouped, fmt, scales):
            count = grouped.shape[1]
            codes = sb(name + "_codes", [P, count, P], U32)
            nc.vector.quantize_mx(
                out=codes[:].rearrange("p i c -> p (i c)").bitcast(fmt),
                scales=scales.rearrange("p i c -> p (i c)"),
                in_=grouped[:].rearrange("p i c t -> p (i c t)"),
            )
            return [(codes[:, i, :], scales[:, i, :]) for i in range(count)]

        def by4(ap):
            return ap.rearrange("p (q t) -> p q t", t=PACK)

        def g_tile(h):
            picked = sb("g_picked%d" % h, [P, J], F32)
            nc.scalar.activation(picked[:], g_win[h][:].indirect(g_list[:]), ACT.Copy)
            rounded = sb("g_rounded%d" % h, [P, J], BF16)
            nc.vector.tensor_tensor(by4(rounded[:]), by4(picked[:]), rb_j, ALU.mult)
            return rounded

        def x_tile(t):
            rounded = sb("x_rounded%d" % t, [P, J], BF16)
            parts = list(zip(CUTS[t], CUTS[t][1:]))
            diffs = []
            for a, (lo, hi) in enumerate(parts):
                diff = sb("diff%d_%d" % (t, a), [P, hi - lo], F32)
                listed = x_win[t][:].indirect(x_list[:, lo // LIST_ROWS : hi // LIST_ROWS])
                if a == 0 and VECTOR_GATHERS_FIRST_PART[t]:
                    nc.vector.tensor_tensor(diff[:], listed, own[t][:, lo:hi], ALU.subtract)
                else:
                    picked = sb("x_picked%d_%d" % (t, a), [P, hi - lo], F32)
                    nc.scalar.activation(picked[:], listed, ACT.Copy)
                    nc.vector.tensor_tensor(diff[:], picked[:], own[t][:, lo:hi], ALU.subtract)
                diffs.append(diff)
            for a, (lo, hi) in enumerate(parts):
                nc.vector.scalar_tensor_tensor(
                    by4(rounded[:, lo:hi]),
                    by4(diffs[a][:]),
                    fk4[:, t : t + 1],
                    ra_j[:, lo // PACK : hi // PACK, :],
                    ALU.mult,
                    ALU.mult,
                )
            return rounded

        w_bank = [psum.tile([P, PACK, P], F32, name="w_bank%d" % h) for h in range(2)]

        x0 = x_tile(0)
        g0 = g_tile(0)
        x1 = x_tile(1)
        g1 = g_tile(1)
        x2 = x_tile(2)
        x3 = x_tile(3)

        x01_grouped = turn("x01", [x0, x1], "x_win3")
        g01_grouped = turn("g01", [g0, g1], "x_picked3_0")
        x2_grouped = turn("x2", [x2], "x_picked3_1")
        x3_grouped = turn("x3", [x3], None)
        first_scales = sb("first_scales", [P, PACK + 2, P], U8, tag="diff3_1")
        uq = quantise("u01", x01_grouped, E4M3, first_scales[:, 0:2, :])
        gq = quantise("g01", g01_grouped, E5M2, first_scales[:, 2:4, :])
        uq = uq + quantise("u2", x2_grouped, E4M3, first_scales[:, 4:5, :])
        uq = uq + quantise("u3", x3_grouped, E4M3, first_scales[:, 5:6, :])
        for t in range(PACK):
            for h in range(2):
                nc.tensor.matmul_mx(
                    out=w_bank[h][:, t, :],
                    lhsT=uq[t][0].bitcast(E4M3),
                    lhsT_scale=uq[t][1],
                    rhs=gq[h][0].bitcast(E5M2),
                    rhs_scale=gq[h][1],
                    start=True,
                    stop=True,
                )

        w_grouped = [sb("w_grouped%d" % h, [P, 1, P, PACK], BF16) for h in range(2)]
        nc.vector.tensor_copy(w_grouped[0][:, 0], w_bank[0][:].rearrange("p t n -> p n t"))
        nc.scalar.copy(w_grouped[1][:, 0], w_bank[1][:].rearrange("p t n -> p n t"))

        v_bank = [psum.tile([P, N], F32, name="v_bank%d" % b) for b in range(2)]
        for h in (1, 0):
            w_scales = sb("w_scales%d" % h, [P, 1, P], U8)
            w_codes, w_bytes = quantise("w%d" % h, w_grouped[h], E5M2, w_scales[:])[0]
            for b in range(2):
                nc.tensor.matmul_mx(
                    out=v_bank[b][:, h * P : (h + 1) * P],
                    lhsT=dr_c[:, b * P : (b + 1) * P].bitcast(E5M2),
                    lhsT_scale=dr_s[:, b * P : (b + 1) * P],
                    rhs=w_codes.bitcast(E5M2),
                    rhs_scale=w_bytes,
                    start=True,
                    stop=True,
                )

        wv = [sb("wv%d" % b, [P, N], F32) for b in range(2)]
        total = [sb("total%d" % b, [P, 1], F32) for b in range(2)]
        mag = [sb("mag%d" % b, [P, N], F32) for b in range(2)]
        mag_sum = [sb("mag_sum%d" % b, [P, 1], F32) for b in range(2)]
        mean = [sb("mean%d" % b, [P, 1], F32) for b in range(2)]
        den = [sb("den%d" % b, [P, 1], F32) for b in range(2)]
        inv = [sb("inv%d" % b, [P, 1], F32) for b in range(2)]
        res = [sb("res%d" % b, [P, N], F32) for b in range(2)]
        for b in range(2):
            nc.vector.scalar_tensor_tensor(
                wv[b][:], v_bank[b][:], 1.0, bn_bc[:], ALU.mult, ALU.add, accum_out=total[b][:]
            )
            nc.scalar.activation(
                mag[b][:],
                wv[b][:],
                ACT.Abs,
                bias=total[b][:],
                scale=-float(N),
                accum_out=mag_sum[b][:],
            )
        for b in range(2):
            nc.vector.tensor_scalar(
                den[b][:], mag_sum[b][:], 1.0 / (N * N), 2.0, ALU.mult, ALU.add
            )
            nc.vector.tensor_scalar(mean[b][:], total[b][:], 1.0 / N, None, ALU.mult)
            nc.vector.reciprocal(inv[b][:], den[b][:])
        for b in range(2):
            nc.vector.tensor_scalar(
                res[b][:], wv[b][:], mean[b][:], inv[b][:], ALU.subtract, ALU.mult
            )
            nc.sync.dma_start(out[b * P : (b + 1) * P, :], res[b][:])
